import numpy as np, ml_dtypes
CORES = [2,34,66,98,130,162,194,226,258,290,322,354,386,418,450,482]
N = 16
TK = 64
def setup_inputs(rng):
    return {"x": rng.standard_normal((N, 128, TK), dtype=np.float32).astype(ml_dtypes.bfloat16), "w": rng.standard_normal((N, 128, 128), dtype=np.float32).astype(ml_dtypes.bfloat16)}
def setup_inputs_big(rng):
    d = setup_inputs(rng)
    for k in ("x", "w"): d[k] = (d[k].astype(np.float32) * 1024.0).astype(d[k].dtype)
    return d
def setup_inputs_small(rng):
    d = setup_inputs(rng)
    for k in ("x", "w"): d[k] = (d[k].astype(np.float32) * (1 / 1024.0)).astype(d[k].dtype)
    return d
def setup_inputs_apart(rng):
    d = setup_inputs(rng)
    f = (10.0 ** rng.permutation(np.linspace(-1.5, 1.5, N))).astype(np.float32).reshape(N, 1, 1)
    for k in ("x", "w"): d[k] = (d[k].astype(np.float32) * f).astype(d[k].dtype)
    return d
def setup_inputs_neg(rng):
    d = setup_inputs(rng)
    d["x"] = (np.abs(d["x"].astype(np.float32)) * 1048576.0).astype(d["x"].dtype); d["w"] = (-np.abs(d["w"].astype(np.float32))).astype(d["w"].dtype)
    return d
def reference(x, w):
    X, W = x.astype(np.float64), w.astype(np.float64)
    y = np.stack([np.max([W[j].T @ X[r] for j in range(N)], axis=0) for r in range(N)])
    return {"y": y.astype(ml_dtypes.bfloat16)}

@@ -1,0 +1,150 @@
+from concourse.bass import DstId, RemoteDMATransfer
+from concourse.mybir import AluOpType
+
+TK = 64
+MW = 128
+
+SCRATCH = {
+    "xd": ("dram", [128, TK], "bfloat16"),
+    "xl": ("dram", [3, 128, TK], "bfloat16"),
+    "xall": ("sbuf", [128, 4 * TK], "bfloat16"),
+    "w0": ("sbuf", [128, MW], "bfloat16"),
+    "w1": ("sbuf", [128, MW], "bfloat16"),
+    "w2": ("sbuf", [128, MW], "bfloat16"),
+    "w3": ("sbuf", [128, MW], "bfloat16"),
+    "p0": ("psum", [128, 512], "float32"),
+    "p1": ("psum", [128, 512], "float32"),
+    "p2": ("psum", [128, 512], "float32"),
+    "p3": ("psum", [128, 512], "float32"),
+    "a0": ("sbuf", [128, 4 * TK], "float32"),
+    "a1": ("sbuf", [128, 4 * TK], "float32"),
+    "a2": ("sbuf", [128, 4 * TK], "float32"),
+    "ys23": ("sbuf", [128, 2 * TK], "bfloat16"),
+    "ys1": ("sbuf", [128, TK], "bfloat16"),
+    "own": ("sbuf", [128, TK], "bfloat16"),
+    "yr1": ("sbuf", [128, TK], "bfloat16"),
+    "yr2": ("sbuf", [128, TK], "bfloat16"),
+    "yr3": ("sbuf", [128, TK], "bfloat16"),
+    "t1": ("sbuf", [128, TK], "bfloat16"),
+    "t2": ("sbuf", [128, TK], "bfloat16"),
+    "yout": ("sbuf", [128, TK], "bfloat16"),
+}
+SEMAPHORES = ["xdl", "wl", "xin", "xa", "wa", "wb", "mm0", "mm1", "mm2", "mm3", "vc", "yv23", "yv1", "vo",
+              "ya1", "ya2", "ya3", "vf", "fin", "st", "sent"]
+
+
+def _groups(core, cores, topo):
+    def rack(c):
+        return topo.rack(topo.host(c))
+
+    def pos(c):
+        return sorted(topo.chip(k) for k in cores if topo.host(k) == topo.host(c)).index(topo.chip(c))
+
+    def hpos(c):
+        return sorted(set(topo.host(k) for k in cores if rack(k) == rack(c))).index(topo.host(c))
+
+    wg, xg = {}, {}
+    for k in cores:
+        if rack(k) == rack(core) and pos(k) // 2 == pos(core) // 2:
+            wg[2 * hpos(k) + pos(k) % 2] = k
+        reach = topo.host(k) == topo.host(core) or (rack(k) != rack(core) and topo.may_write(core, k))
+        if reach and pos(k) % 2 == pos(core) % 2:
+            xg[2 * rack(k) + pos(k) // 2] = k
+    wi = [i for i in wg if wg[i] == core][0]
+    xi = [i for i in xg if xg[i] == core][0]
+    return {e: wg[wi ^ e] for e in range(4)}, {d: xg[xi ^ d] for d in range(4)}
+
+
+def rank_program(g, core, T, topo):
+    if T.rank_of(core) is None:
+        return
+    S = T.sem
+    wg, xg = _groups(core, list(T.cores), topo)
+
+    def dst(c):
+        rid, pid = topo.addr(c, core)
+        return DstId(rid=rid, pnc=pid)
+
+    full = topo.mask(core, wg[1])
+    for c in [wg[2], wg[3], xg[1], xg[2], xg[3]]:
+        full &= topo.mask(core, c)
+    eng = [b for b in range(16) if (full >> b) & 1]
+    ne = len(eng)
+    lo = sum(1 << b for b in eng[: ne // 2])
+    hi = sum(1 << b for b in eng[ne // 2:])
+
+    def blk(d):
+        return slice(d * TK, (d + 1) * TK)
+
+    g.sync.dma_start(T.xd[:], T.x[:]).then_inc(S.xdl, 16)
+    g.scalar.dma_start(T.w0[:], T.w[:]).then_inc(S.wl, 16)
+    g.sync.dma_start(T.xall[:, blk(0)], T.x[:]).then_inc(S.xin, 16)
+
+    order = [3, 2, 1]
+    g.wait_ge(S.xdl, 16)
+    g.remote_dma_fused([RemoteDMATransfer(dst_ids=[dst(xg[d]) for d in order], dma_engine_mask=full, remote_sem=S.xa,
+                                          srcs=[T.xd[:]], dsts=[T.xl[d - 1] for d in order], alu_op=0)], local_sem=S.sent)
+    g.wait_ge(S.wl, 16)
+    g.remote_dma_fused([RemoteDMATransfer(dst_ids=[dst(wg[1]), dst(wg[2])], dma_engine_mask=full, remote_sem=S.wa,
+                                          srcs=[T.w0[:]], dsts=[T.w1[:], T.w2[:]], alu_op=0)], local_sem=S.sent)
+    rid, pid = topo.addr(wg[3], core)
+    g.remote_dma(T.w3[:], T.w0[:], S.wb, S.sent, pid, rid, full)
+
+    g.scalar.wait_ge(S.xa, 3 * ne)
+    g.sync.wait_ge(S.xa, 3 * ne)
+    g.scalar.dma_start(T.xall[:, blk(3)], T.xl[2]).then_inc(S.xin, 16)
+    g.sync.dma_start(T.xall[:, blk(2)], T.xl[1]).then_inc(S.xin, 16)
+    g.scalar.dma_start(T.xall[:, blk(1)], T.xl[0]).then_inc(S.xin, 16)
+
+    n = 4 * TK
+    te = g.tensor
+    te.wait_ge(S.xin, 64)
+    te.wait_ge(S.wl, 16)
+    te.matmul(T.p0[:, 0:n], T.w0[:], T.xall[:], start=True, stop=True).then_inc(S.mm0, 1)
+    te.wait_ge(S.wa, 2 * ne)
+    te.matmul(T.p1[:, 0:n], T.w1[:], T.xall[:], start=True, stop=True).then_inc(S.mm1, 1)
+    te.matmul(T.p2[:, 0:n], T.w2[:], T.xall[:], start=True, stop=True).then_inc(S.mm2, 1)
+    te.wait_ge(S.wb, ne)
+    te.matmul(T.p3[:, 0:n], T.w3[:], T.xall[:], start=True, stop=True).then_inc(S.mm3, 1)
+
+    ve = g.vector
+    mx = AluOpType.max
+    ve.wait_ge(S.mm0, 1)
+    ve.tensor_copy(T.a0[:], T.p0[:, 0:n]).then_inc(S.vc, 1)
+    ve.wait_ge(S.mm1, 1)
+    ve.wait_ge(S.vc, 1)
+    ve.tensor_tensor(T.a1[:], T.a0[:], T.p1[:, 0:n], mx).then_inc(S.vc, 1)
+    ve.wait_ge(S.mm2, 1)
+    ve.wait_ge(S.vc, 2)
+    ve.tensor_tensor(T.a2[:], T.a1[:], T.p2[:, 0:n], mx).then_inc(S.vc, 1)
+    ve.wait_ge(S.mm3, 1)
+    ve.wait_ge(S.vc, 3)
+    ve.tensor_tensor(T.ys23[:], T.a2[:, 2 * TK:4 * TK], T.p3[:, 2 * TK:4 * TK], mx).then_inc(S.yv23, 1)
+    ve.tensor_tensor(T.ys1[:], T.a2[:, blk(1)], T.p3[:, blk(1)], mx).then_inc(S.yv1, 1)
+    ve.tensor_tensor(T.own[:], T.a2[:, blk(0)], T.p3[:, blk(0)], mx).then_inc(S.vo, 1)
+
+    g.wait_ge(S.yv23, 1)
+    g.remote_dma_fused([
+        RemoteDMATransfer(dst_ids=[dst(xg[3])], dma_engine_mask=lo, remote_sem=S.ya3,
+                          srcs=[T.ys23[:, TK:2 * TK]], dsts=[T.yr3[:]], alu_op=0),
+        RemoteDMATransfer(dst_ids=[dst(xg[2])], dma_engine_mask=hi, remote_sem=S.ya2,
+                          srcs=[T.ys23[:, 0:TK]], dsts=[T.yr2[:]], alu_op=0),
+    ], local_sem=S.sent)
+    g.wait_ge(S.yv1, 1)
+    rid, pid = topo.addr(xg[1], core)
+    g.remote_dma(T.yr1[:], T.ys1[:], S.ya1, S.sent, pid, rid, full)
+
+    ve.wait_ge(S.vo, 1)
+    ve.wait_ge(S.ya2, ne // 2)
+    ve.tensor_tensor(T.t1[:], T.own[:], T.yr2[:], mx).then_inc(S.vf, 1)
+    ve.wait_ge(S.ya3, ne // 2)
+    ve.wait_ge(S.vf, 1)
+    ve.tensor_tensor(T.t2[:], T.t1[:], T.yr3[:], mx).then_inc(S.vf, 1)
+    ve.wait_ge(S.ya1, ne)
+    ve.wait_ge(S.vf, 2)
+    ve.tensor_tensor(T.yout[:], T.t2[:], T.yr1[:], mx).then_inc(S.fin, 1)
+
+    g.sync.wait_ge(S.fin, 1)
+    g.sync.dma_start(T.y[:], T.yout[:]).then_inc(S.st, 16)
+    g.sync.wait_ge(S.st, 16)
+    g.wait_ge(S.sent, 5 * ne)

@@ -5,8 +5,6 @@ TK = 64
 MW = 128
 
 SCRATCH = {
-    "xd": ("dram", [128, TK], "bfloat16"),
-    "xl": ("dram", [3, 128, TK], "bfloat16"),
     "xall": ("sbuf", [128, 4 * TK], "bfloat16"),
     "w0": ("sbuf", [128, MW], "bfloat16"),
     "w1": ("sbuf", [128, MW], "bfloat16"),
@@ -16,9 +14,13 @@ SCRATCH = {
     "p1": ("psum", [128, 512], "float32"),
     "p2": ("psum", [128, 512], "float32"),
     "p3": ("psum", [128, 512], "float32"),
+    "p4": ("psum", [128, 512], "float32"),
     "a0": ("sbuf", [128, 4 * TK], "float32"),
     "a1": ("sbuf", [128, 4 * TK], "float32"),
     "a2": ("sbuf", [128, 4 * TK], "float32"),
+    "o0": ("sbuf", [128, TK], "float32"),
+    "o1": ("sbuf", [128, TK], "float32"),
+    "o2": ("sbuf", [128, TK], "float32"),
     "ys23": ("sbuf", [128, 2 * TK], "bfloat16"),
     "ys1": ("sbuf", [128, TK], "bfloat16"),
     "own": ("sbuf", [128, TK], "bfloat16"),
@@ -29,7 +31,7 @@ SCRATCH = {
     "t2": ("sbuf", [128, TK], "bfloat16"),
     "yout": ("sbuf", [128, TK], "bfloat16"),
 }
-SEMAPHORES = ["xdl", "wl", "xin", "xa", "wa", "wb", "mm0", "mm1", "mm2", "mm3", "vc", "yv23", "yv1", "vo",
+SEMAPHORES = ["wl", "xin", "xa", "wa", "wb", "mm0", "mm1", "mm2", "mm3", "mm4", "vc", "yv23", "yv1", "vo",
               "ya1", "ya2", "ya3", "vf", "fin", "st", "sent"]
 
 
@@ -76,52 +78,59 @@ def rank_program(g, core, T, topo):
     def blk(d):
         return slice(d * TK, (d + 1) * TK)
 
-    g.sync.dma_start(T.xd[:], T.x[:]).then_inc(S.xdl, 16)
-    g.scalar.dma_start(T.w0[:], T.w[:]).then_inc(S.wl, 16)
+    n = 4 * TK
+    far = slice(2 * TK, n)
+    near = slice(0, 2 * TK)
+    frn = slice(TK, n)
+
     g.sync.dma_start(T.xall[:, blk(0)], T.x[:]).then_inc(S.xin, 16)
+    g.scalar.dma_start(T.w0[:], T.w[:]).then_inc(S.wl, 16)
 
     order = [3, 2, 1]
-    g.wait_ge(S.xdl, 16)
+    g.wait_ge(S.xin, 16)
     g.remote_dma_fused([RemoteDMATransfer(dst_ids=[dst(xg[d]) for d in order], dma_engine_mask=full, remote_sem=S.xa,
-                                          srcs=[T.xd[:]], dsts=[T.xl[d - 1] for d in order], alu_op=0)], local_sem=S.sent)
+                                          srcs=[T.xall[:, blk(0)]], dsts=[T.xall[:, blk(d)] for d in order], alu_op=0)],
+                       local_sem=S.sent)
     g.wait_ge(S.wl, 16)
     g.remote_dma_fused([RemoteDMATransfer(dst_ids=[dst(wg[1]), dst(wg[2])], dma_engine_mask=full, remote_sem=S.wa,
                                           srcs=[T.w0[:]], dsts=[T.w1[:], T.w2[:]], alu_op=0)], local_sem=S.sent)
     rid, pid = topo.addr(wg[3], core)
     g.remote_dma(T.w3[:], T.w0[:], S.wb, S.sent, pid, rid, full)
 
-    g.scalar.wait_ge(S.xa, 3 * ne)
-    g.sync.wait_ge(S.xa, 3 * ne)
-    g.scalar.dma_start(T.xall[:, blk(3)], T.xl[2]).then_inc(S.xin, 16)
-    g.sync.dma_start(T.xall[:, blk(2)], T.xl[1]).then_inc(S.xin, 16)
-    g.scalar.dma_start(T.xall[:, blk(1)], T.xl[0]).then_inc(S.xin, 16)
-
-    n = 4 * TK
     te = g.tensor
-    te.wait_ge(S.xin, 64)
+    te.wait_ge(S.xin, 16)
+    te.wait_ge(S.xa, 3 * ne)
     te.wait_ge(S.wl, 16)
     te.matmul(T.p0[:, 0:n], T.w0[:], T.xall[:], start=True, stop=True).then_inc(S.mm0, 1)
     te.wait_ge(S.wa, 2 * ne)
     te.matmul(T.p1[:, 0:n], T.w1[:], T.xall[:], start=True, stop=True).then_inc(S.mm1, 1)
     te.matmul(T.p2[:, 0:n], T.w2[:], T.xall[:], start=True, stop=True).then_inc(S.mm2, 1)
     te.wait_ge(S.wb, ne)
-    te.matmul(T.p3[:, 0:n], T.w3[:], T.xall[:], start=True, stop=True).then_inc(S.mm3, 1)
+    te.matmul(T.p3[:, far], T.w3[:], T.xall[:, far], start=True, stop=True).then_inc(S.mm3, 1)
+    te.matmul(T.p4[:, near], T.w3[:], T.xall[:, near], start=True, stop=True).then_inc(S.mm4, 1)
 
     ve = g.vector
     mx = AluOpType.max
     ve.wait_ge(S.mm0, 1)
-    ve.tensor_copy(T.a0[:], T.p0[:, 0:n]).then_inc(S.vc, 1)
+    ve.tensor_copy(T.a0[:, frn], T.p0[:, frn]).then_inc(S.vc, 1)
     ve.wait_ge(S.mm1, 1)
     ve.wait_ge(S.vc, 1)
-    ve.tensor_tensor(T.a1[:], T.a0[:], T.p1[:, 0:n], mx).then_inc(S.vc, 1)
+    ve.tensor_tensor(T.a1[:, frn], T.a0[:, frn], T.p1[:, frn], mx).then_inc(S.vc, 1)
     ve.wait_ge(S.mm2, 1)
     ve.wait_ge(S.vc, 2)
-    ve.tensor_tensor(T.a2[:], T.a1[:], T.p2[:, 0:n], mx).then_inc(S.vc, 1)
+    ve.tensor_tensor(T.a2[:, frn], T.a1[:, frn], T.p2[:, frn], mx).then_inc(S.vc, 1)
     ve.wait_ge(S.mm3, 1)
     ve.wait_ge(S.vc, 3)
-    ve.tensor_tensor(T.ys23[:], T.a2[:, 2 * TK:4 * TK], T.p3[:, 2 * TK:4 * TK], mx).then_inc(S.yv23, 1)
-    ve.tensor_tensor(T.ys1[:], T.a2[:, blk(1)], T.p3[:, blk(1)], mx).then_inc(S.yv1, 1)
-    ve.tensor_tensor(T.own[:], T.a2[:, blk(0)], T.p3[:, blk(0)], mx).then_inc(S.vo, 1)
+    ve.tensor_tensor(T.ys23[:], T.a2[:, far], T.p3[:, far], mx).then_inc(S.yv23, 1)
+    ve.wait_ge(S.mm4, 1)
+    ve.tensor_tensor(T.ys1[:], T.a2[:, blk(1)], T.p4[:, blk(1)], mx).then_inc(S.yv1, 1)
+    ve.tensor_copy(T.o0[:], T.p0[:, blk(0)]).then_inc(S.vo, 1)
+    ve.wait_ge(S.vo, 1)
+    ve.tensor_tensor(T.o1[:], T.o0[:], T.p1[:, blk(0)], mx).then_inc(S.vo, 1)
+    ve.wait_ge(S.vo, 2)
+    ve.tensor_tensor(T.o2[:], T.o1[:], T.p2[:, blk(0)], mx).then_inc(S.vo, 1)
+    ve.wait_ge(S.vo, 3)
+    ve.tensor_tensor(T.own[:], T.o2[:], T.p4[:, blk(0)], mx).then_inc(S.vo, 1)
 
     g.wait_ge(S.yv23, 1)
     g.remote_dma_fused([
@@ -134,7 +143,7 @@ def rank_program(g, core, T, topo):
     rid, pid = topo.addr(xg[1], core)
     g.remote_dma(T.yr1[:], T.ys1[:], S.ya1, S.sent, pid, rid, full)
 
-    ve.wait_ge(S.vo, 1)
+    ve.wait_ge(S.vo, 4)
     ve.wait_ge(S.ya2, ne // 2)
     ve.tensor_tensor(T.t1[:], T.own[:], T.yr2[:], mx).then_inc(S.vf, 1)
     ve.wait_ge(S.ya3, ne // 2)

@@ -5,34 +5,41 @@ TK = 64
 MW = 128
 
 SCRATCH = {
-    "xall": ("sbuf", [128, 4 * TK], "bfloat16"),
+    "xall": ("sbuf", [128, 3 * TK], "bfloat16"),
     "w0": ("sbuf", [128, MW], "bfloat16"),
     "w1": ("sbuf", [128, MW], "bfloat16"),
     "w2": ("sbuf", [128, MW], "bfloat16"),
     "w3": ("sbuf", [128, MW], "bfloat16"),
-    "p0": ("psum", [128, 512], "float32"),
-    "p1": ("psum", [128, 512], "float32"),
-    "p2": ("psum", [128, 512], "float32"),
-    "p3": ("psum", [128, 512], "float32"),
-    "p4": ("psum", [128, 512], "float32"),
-    "a0": ("sbuf", [128, 4 * TK], "float32"),
-    "a1": ("sbuf", [128, 4 * TK], "float32"),
-    "a2": ("sbuf", [128, 4 * TK], "float32"),
-    "o0": ("sbuf", [128, TK], "float32"),
-    "o1": ("sbuf", [128, TK], "float32"),
-    "o2": ("sbuf", [128, TK], "float32"),
-    "ys23": ("sbuf", [128, 2 * TK], "bfloat16"),
-    "ys1": ("sbuf", [128, TK], "bfloat16"),
+    "v0": ("sbuf", [128, MW], "bfloat16"),
+    "v1": ("sbuf", [128, MW], "bfloat16"),
+    "v2": ("sbuf", [128, MW], "bfloat16"),
+    "v3": ("sbuf", [128, MW], "bfloat16"),
+    "wd": ("dram", [128, MW], "bfloat16"),
+    "f0": ("psum", [128, 512], "float32"),
+    "f1": ("psum", [128, 512], "float32"),
+    "f2": ("psum", [128, 512], "float32"),
+    "f3a": ("psum", [128, 512], "float32"),
+    "f3b": ("psum", [128, 512], "float32"),
+    "px": ("psum", [128, 512], "float32"),
+    "pa": ("psum", [128, 512], "float32"),
+    "pb": ("psum", [128, 512], "float32"),
+    "a0": ("sbuf", [128, 2 * TK], "float32"),
+    "a1": ("sbuf", [128, 2 * TK], "float32"),
+    "a2": ("sbuf", [128, 2 * TK], "float32"),
+    "o1": ("sbuf", [128, 2 * TK], "float32"),
+    "o2": ("sbuf", [128, 2 * TK], "float32"),
+    "o3": ("sbuf", [128, 2 * TK], "float32"),
+    "o4": ("sbuf", [128, 2 * TK], "float32"),
+    "ys2": ("sbuf", [128, TK], "bfloat16"),
+    "ys3": ("sbuf", [128, TK], "bfloat16"),
     "own": ("sbuf", [128, TK], "bfloat16"),
-    "yr1": ("sbuf", [128, TK], "bfloat16"),
     "yr2": ("sbuf", [128, TK], "bfloat16"),
     "yr3": ("sbuf", [128, TK], "bfloat16"),
     "t1": ("sbuf", [128, TK], "bfloat16"),
-    "t2": ("sbuf", [128, TK], "bfloat16"),
     "yout": ("sbuf", [128, TK], "bfloat16"),
 }
-SEMAPHORES = ["wl", "xin", "xa", "wa", "wb", "mm0", "mm1", "mm2", "mm3", "mm4", "vc", "yv23", "yv1", "vo",
-              "ya1", "ya2", "ya3", "vf", "fin", "st", "sent"]
+SEMAPHORES = ["wl", "wdl", "xin", "xa", "wa", "wc", "wb", "hw", "la", "lb", "mf0", "mf1", "mf2", "mf3a", "mf3b", "mx", "ma",
+              "mb", "vc", "yv2", "yv3", "vo", "ya2", "ya3", "vf", "fin", "st", "sent"]
 
 
 def _groups(core, cores, topo):
@@ -57,103 +64,145 @@ def _groups(core, cores, topo):
     return {e: wg[wi ^ e] for e in range(4)}, {d: xg[xi ^ d] for d in range(4)}
 
 
+def _count(m):
+    return sum((m >> b) & 1 for b in range(m.bit_length()))
+
+
 def rank_program(g, core, T, topo):
-    if T.rank_of(core) is None:
-        return
+    cores = list(T.cores)
     S = T.sem
-    wg, xg = _groups(core, list(T.cores), topo)
+    home = [k for k in cores if topo.host(k) == topo.host(core) and topo.chip(k) == topo.chip(core)]
+    if not home:
+        return
+    rank = home[0]
+    wg, xg = _groups(rank, cores, topo)
+    og = _groups(xg[1], cores, topo)[0]
+    total = (max(topo.host(k) for k in cores) + 1) * topo.CORES_PER_HOST
+    helpers = [c for c in range(total)
+               if topo.host(c) == topo.host(rank) and topo.chip(c) == topo.chip(rank) and c != rank
+               and topo.die(c) != topo.die(rank) and topo.may_write(rank, c)
+               and all(topo.may_write(c, og[e]) for e in og)][:2]
+
+    full = topo.mask(rank, wg[1])
+    for c in [wg[2], wg[3], xg[2], xg[3], og[3]]:
+        full &= topo.mask(rank, c)
+    ne = _count(full)
+    onm = ~full
+    for h in helpers:
+        onm &= topo.mask(rank, h)
+    non = _count(onm)
+    hm = topo.mask(helpers[0], og[0])
+    for h in helpers:
+        for e in og:
+            hm &= topo.mask(h, og[e])
+    nh = _count(hm)
+
+    if core != rank:
+        if core not in helpers:
+            return
+        jobs = [[(0, S.la), (1, S.lb)], [(2, S.la)]][helpers.index(core)]
+        g.wait_ge(S.hw, non)
+        for e, sem in jobs:
+            rid, pid = topo.addr(og[e], core)
+            g.remote_dma(T["v%d" % e][:], T.wd[:], sem, S.sent, pid, rid, hm)
+        g.wait_ge(S.sent, len(jobs) * nh)
+        return
 
     def dst(c):
         rid, pid = topo.addr(c, core)
         return DstId(rid=rid, pnc=pid)
 
-    full = topo.mask(core, wg[1])
-    for c in [wg[2], wg[3], xg[1], xg[2], xg[3]]:
-        full &= topo.mask(core, c)
-    eng = [b for b in range(16) if (full >> b) & 1]
-    ne = len(eng)
-    lo = sum(1 << b for b in eng[: ne // 2])
-    hi = sum(1 << b for b in eng[ne // 2:])
-
     def blk(d):
         return slice(d * TK, (d + 1) * TK)
 
-    n = 4 * TK
-    far = slice(2 * TK, n)
-    near = slice(0, 2 * TK)
-    frn = slice(TK, n)
+    frn = slice(TK, 3 * TK)
+    n2 = 2 * TK
+    lo, hi = slice(0, TK), slice(TK, n2)
 
     g.sync.dma_start(T.xall[:, blk(0)], T.x[:]).then_inc(S.xin, 16)
     g.scalar.dma_start(T.w0[:], T.w[:]).then_inc(S.wl, 16)
+    g.sync.dma_start(T.wd[:], T.w[:]).then_inc(S.wdl, 16)
 
-    order = [3, 2, 1]
     g.wait_ge(S.xin, 16)
-    g.remote_dma_fused([RemoteDMATransfer(dst_ids=[dst(xg[d]) for d in order], dma_engine_mask=full, remote_sem=S.xa,
-                                          srcs=[T.xall[:, blk(0)]], dsts=[T.xall[:, blk(d)] for d in order], alu_op=0)],
+    g.remote_dma_fused([RemoteDMATransfer(dst_ids=[dst(xg[3]), dst(xg[2])], dma_engine_mask=full, remote_sem=S.xa,
+                                          srcs=[T.xall[:, blk(0)]], dsts=[T.xall[:, blk(2)], T.xall[:, blk(1)]], alu_op=0)],
                        local_sem=S.sent)
+    g.wait_ge(S.wdl, 16)
+    g.remote_dma_fused([RemoteDMATransfer(dst_ids=[dst(h) for h in helpers], dma_engine_mask=onm, remote_sem=S.hw,
+                                          srcs=[T.wd[:]], dsts=[T.wd[:] for h in helpers], alu_op=0)], local_sem=S.sent)
     g.wait_ge(S.wl, 16)
-    g.remote_dma_fused([RemoteDMATransfer(dst_ids=[dst(wg[1]), dst(wg[2])], dma_engine_mask=full, remote_sem=S.wa,
-                                          srcs=[T.w0[:]], dsts=[T.w1[:], T.w2[:]], alu_op=0)], local_sem=S.sent)
-    rid, pid = topo.addr(wg[3], core)
-    g.remote_dma(T.w3[:], T.w0[:], S.wb, S.sent, pid, rid, full)
+    for c, buf, sem in ((wg[1], T.w1, S.wa), (wg[2], T.w2, S.wc), (wg[3], T.w3, S.wb), (og[3], T.v3, S.lb)):
+        rid, pid = topo.addr(c, core)
+        g.remote_dma(buf[:], T.w0[:], sem, S.sent, pid, rid, full)
 
     te = g.tensor
+    xo = T.xall[:, blk(0)]
+    xf = T.xall[:, frn]
     te.wait_ge(S.xin, 16)
-    te.wait_ge(S.xa, 3 * ne)
+    te.wait_ge(S.xa, 2 * ne)
     te.wait_ge(S.wl, 16)
-    te.matmul(T.p0[:, 0:n], T.w0[:], T.xall[:], start=True, stop=True).then_inc(S.mm0, 1)
-    te.wait_ge(S.wa, 2 * ne)
-    te.matmul(T.p1[:, 0:n], T.w1[:], T.xall[:], start=True, stop=True).then_inc(S.mm1, 1)
-    te.matmul(T.p2[:, 0:n], T.w2[:], T.xall[:], start=True, stop=True).then_inc(S.mm2, 1)
+    te.matmul(T.f0[:, 0:n2], T.w0[:], xf, start=True, stop=True).then_inc(S.mf0, 1)
+    te.matmul(T.px[:, blk(0)], T.w0[:], xo, start=True, stop=True).then_inc(S.mx, 1)
+    te.wait_ge(S.wa, ne)
+    te.matmul(T.f1[:, 0:n2], T.w1[:], xf, start=True, stop=True).then_inc(S.mf1, 1)
+    te.wait_ge(S.wc, ne)
+    te.matmul(T.f2[:, 0:n2], T.w2[:], xf, start=True, stop=True).then_inc(S.mf2, 1)
     te.wait_ge(S.wb, ne)
-    te.matmul(T.p3[:, far], T.w3[:], T.xall[:, far], start=True, stop=True).then_inc(S.mm3, 1)
-    te.matmul(T.p4[:, near], T.w3[:], T.xall[:, near], start=True, stop=True).then_inc(S.mm4, 1)
+    te.matmul(T.f3a[:, lo], T.w3[:], T.xall[:, blk(2)], start=True, stop=True).then_inc(S.mf3a, 1)
+    te.matmul(T.f3b[:, lo], T.w3[:], T.xall[:, blk(1)], start=True, stop=True).then_inc(S.mf3b, 1)
+    te.matmul(T.px[:, blk(1)], T.w1[:], xo, start=True, stop=True).then_inc(S.mx, 1)
+    te.matmul(T.px[:, blk(2)], T.w2[:], xo, start=True, stop=True).then_inc(S.mx, 1)
+    te.matmul(T.px[:, blk(3)], T.w3[:], xo, start=True, stop=True).then_inc(S.mx, 1)
+    te.wait_ge(S.la, 2 * nh)
+    te.matmul(T.pa[:, lo], T.v0[:], xo, start=True, stop=True).then_inc(S.ma, 1)
+    te.matmul(T.pa[:, hi], T.v2[:], xo, start=True, stop=True).then_inc(S.ma, 1)
+    te.wait_ge(S.lb, nh + ne)
+    te.matmul(T.pb[:, lo], T.v1[:], xo, start=True, stop=True).then_inc(S.mb, 1)
+    te.matmul(T.pb[:, hi], T.v3[:], xo, start=True, stop=True).then_inc(S.mb, 1)
 
     ve = g.vector
     mx = AluOpType.max
-    ve.wait_ge(S.mm0, 1)
-    ve.tensor_copy(T.a0[:, frn], T.p0[:, frn]).then_inc(S.vc, 1)
-    ve.wait_ge(S.mm1, 1)
+    ve.wait_ge(S.mf0, 1)
+    ve.tensor_copy(T.a0[:], T.f0[:, 0:n2]).then_inc(S.vc, 1)
+    ve.wait_ge(S.mf1, 1)
     ve.wait_ge(S.vc, 1)
-    ve.tensor_tensor(T.a1[:, frn], T.a0[:, frn], T.p1[:, frn], mx).then_inc(S.vc, 1)
-    ve.wait_ge(S.mm2, 1)
+    ve.tensor_tensor(T.a1[:], T.a0[:], T.f1[:, 0:n2], mx).then_inc(S.vc, 1)
+    ve.wait_ge(S.mf2, 1)
     ve.wait_ge(S.vc, 2)
-    ve.tensor_tensor(T.a2[:, frn], T.a1[:, frn], T.p2[:, frn], mx).then_inc(S.vc, 1)
-    ve.wait_ge(S.mm3, 1)
+    ve.tensor_tensor(T.a2[:], T.a1[:], T.f2[:, 0:n2], mx).then_inc(S.vc, 1)
+    ve.wait_ge(S.mf3a, 1)
     ve.wait_ge(S.vc, 3)
-    ve.tensor_tensor(T.ys23[:], T.a2[:, far], T.p3[:, far], mx).then_inc(S.yv23, 1)
-    ve.wait_ge(S.mm4, 1)
-    ve.tensor_tensor(T.ys1[:], T.a2[:, blk(1)], T.p4[:, blk(1)], mx).then_inc(S.yv1, 1)
-    ve.tensor_copy(T.o0[:], T.p0[:, blk(0)]).then_inc(S.vo, 1)
+    ve.tensor_tensor(T.ys3[:], T.a2[:, hi], T.f3a[:, lo], mx).then_inc(S.yv3, 1)
+    ve.wait_ge(S.mf3b, 1)
+    ve.tensor_tensor(T.ys2[:], T.a2[:, lo], T.f3b[:, lo], mx).then_inc(S.yv2, 1)
+    ve.wait_ge(S.mx, 4)
+    ve.tensor_copy(T.o1[:], T.px[:, 0:n2]).then_inc(S.vo, 1)
     ve.wait_ge(S.vo, 1)
-    ve.tensor_tensor(T.o1[:], T.o0[:], T.p1[:, blk(0)], mx).then_inc(S.vo, 1)
+    ve.tensor_tensor(T.o2[:], T.o1[:], T.px[:, n2:2 * n2], mx).then_inc(S.vo, 1)
+    ve.wait_ge(S.ma, 2)
     ve.wait_ge(S.vo, 2)
-    ve.tensor_tensor(T.o2[:], T.o1[:], T.p2[:, blk(0)], mx).then_inc(S.vo, 1)
+    ve.tensor_tensor(T.o3[:], T.o2[:], T.pa[:, 0:n2], mx).then_inc(S.vo, 1)
+    ve.wait_ge(S.mb, 2)
     ve.wait_ge(S.vo, 3)
-    ve.tensor_tensor(T.own[:], T.o2[:], T.p4[:, blk(0)], mx).then_inc(S.vo, 1)
-
-    g.wait_ge(S.yv23, 1)
-    g.remote_dma_fused([
-        RemoteDMATransfer(dst_ids=[dst(xg[3])], dma_engine_mask=lo, remote_sem=S.ya3,
-                          srcs=[T.ys23[:, TK:2 * TK]], dsts=[T.yr3[:]], alu_op=0),
-        RemoteDMATransfer(dst_ids=[dst(xg[2])], dma_engine_mask=hi, remote_sem=S.ya2,
-                          srcs=[T.ys23[:, 0:TK]], dsts=[T.yr2[:]], alu_op=0),
-    ], local_sem=S.sent)
-    g.wait_ge(S.yv1, 1)
-    rid, pid = topo.addr(xg[1], core)
-    g.remote_dma(T.yr1[:], T.ys1[:], S.ya1, S.sent, pid, rid, full)
-
+    ve.tensor_tensor(T.o4[:], T.o3[:], T.pb[:, 0:n2], mx).then_inc(S.vo, 1)
     ve.wait_ge(S.vo, 4)
-    ve.wait_ge(S.ya2, ne // 2)
-    ve.tensor_tensor(T.t1[:], T.own[:], T.yr2[:], mx).then_inc(S.vf, 1)
-    ve.wait_ge(S.ya3, ne // 2)
+    ve.tensor_tensor(T.own[:], T.o4[:, lo], T.o4[:, hi], mx).then_inc(S.vo, 1)
+
+    g.wait_ge(S.yv3, 1)
+    rid, pid = topo.addr(xg[3], core)
+    g.remote_dma(T.yr3[:], T.ys3[:], S.ya3, S.sent, pid, rid, full)
+    g.wait_ge(S.yv2, 1)
+    rid, pid = topo.addr(xg[2], core)
+    g.remote_dma(T.yr2[:], T.ys2[:], S.ya2, S.sent, pid, rid, full)
+
+    ve.wait_ge(S.vo, 5)
+    ve.wait_ge(S.ya3, ne)
+    ve.tensor_tensor(T.t1[:], T.own[:], T.yr3[:], mx).then_inc(S.vf, 1)
+    ve.wait_ge(S.ya2, ne)
     ve.wait_ge(S.vf, 1)
-    ve.tensor_tensor(T.t2[:], T.t1[:], T.yr3[:], mx).then_inc(S.vf, 1)
-    ve.wait_ge(S.ya1, ne)
-    ve.wait_ge(S.vf, 2)
-    ve.tensor_tensor(T.yout[:], T.t2[:], T.yr1[:], mx).then_inc(S.fin, 1)
+    ve.tensor_tensor(T.yout[:], T.t1[:], T.yr2[:], mx).then_inc(S.fin, 1)
 
     g.sync.wait_ge(S.fin, 1)
     g.sync.dma_start(T.y[:], T.yout[:]).then_inc(S.st, 16)
     g.sync.wait_ge(S.st, 16)
-    g.wait_ge(S.sent, 5 * ne)
+    g.wait_ge(S.sent, 7 * ne + non)

from concourse.bass import DstId, RemoteDMATransfer
from concourse.mybir import AluOpType

TK = 64
MW = 128

SCRATCH = {
    "xall": ("sbuf", [128, 3 * TK], "bfloat16"),
    "w0": ("sbuf", [128, MW], "bfloat16"),
    "w1": ("sbuf", [128, MW], "bfloat16"),
    "w2": ("sbuf", [128, MW], "bfloat16"),
    "w3": ("sbuf", [128, MW], "bfloat16"),
    "v0": ("sbuf", [128, MW], "bfloat16"),
    "v1": ("sbuf", [128, MW], "bfloat16"),
    "v2": ("sbuf", [128, MW], "bfloat16"),
    "v3": ("sbuf", [128, MW], "bfloat16"),
    "wd": ("dram", [128, MW], "bfloat16"),
    "f0": ("psum", [128, 512], "float32"),
    "f1": ("psum", [128, 512], "float32"),
    "f2": ("psum", [128, 512], "float32"),
    "f3a": ("psum", [128, 512], "float32"),
    "f3b": ("psum", [128, 512], "float32"),
    "px": ("psum", [128, 512], "float32"),
    "pa": ("psum", [128, 512], "float32"),
    "pb": ("psum", [128, 512], "float32"),
    "a0": ("sbuf", [128, 2 * TK], "float32"),
    "a1": ("sbuf", [128, 2 * TK], "float32"),
    "a2": ("sbuf", [128, 2 * TK], "float32"),
    "o1": ("sbuf", [128, 2 * TK], "float32"),
    "o2": ("sbuf", [128, 2 * TK], "float32"),
    "o3": ("sbuf", [128, 2 * TK], "float32"),
    "o4": ("sbuf", [128, 2 * TK], "float32"),
    "ys2": ("sbuf", [128, TK], "bfloat16"),
    "ys3": ("sbuf", [128, TK], "bfloat16"),
    "own": ("sbuf", [128, TK], "bfloat16"),
    "yr2": ("sbuf", [128, TK], "bfloat16"),
    "yr3": ("sbuf", [128, TK], "bfloat16"),
    "t1": ("sbuf", [128, TK], "bfloat16"),
    "yout": ("sbuf", [128, TK], "bfloat16"),
}
SEMAPHORES = ["wl", "wdl", "xin", "xa", "wa", "wc", "wb", "hw", "la", "lb", "mf0", "mf1", "mf2", "mf3a", "mf3b", "mx", "ma",
              "mb", "vc", "yv2", "yv3", "vo", "ya2", "ya3", "vf", "fin", "st", "sent"]


def _groups(core, cores, topo):
    def rack(c):
        return topo.rack(topo.host(c))

    def pos(c):
        return sorted(topo.chip(k) for k in cores if topo.host(k) == topo.host(c)).index(topo.chip(c))

    def hpos(c):
        return sorted(set(topo.host(k) for k in cores if rack(k) == rack(c))).index(topo.host(c))

    wg, xg = {}, {}
    for k in cores:
        if rack(k) == rack(core) and pos(k) // 2 == pos(core) // 2:
            wg[2 * hpos(k) + pos(k) % 2] = k
        reach = topo.host(k) == topo.host(core) or (rack(k) != rack(core) and topo.may_write(core, k))
        if reach and pos(k) % 2 == pos(core) % 2:
            xg[2 * rack(k) + pos(k) // 2] = k
    wi = [i for i in wg if wg[i] == core][0]
    xi = [i for i in xg if xg[i] == core][0]
    return {e: wg[wi ^ e] for e in range(4)}, {d: xg[xi ^ d] for d in range(4)}


def _count(m):
    return sum((m >> b) & 1 for b in range(m.bit_length()))


def rank_program(g, core, T, topo):
    cores = list(T.cores)
    S = T.sem
    home = [k for k in cores if topo.host(k) == topo.host(core) and topo.chip(k) == topo.chip(core)]
    if not home:
        return
    rank = home[0]
    wg, xg = _groups(rank, cores, topo)
    og = _groups(xg[1], cores, topo)[0]
    total = (max(topo.host(k) for k in cores) + 1) * topo.CORES_PER_HOST
    helpers = [c for c in range(total)
               if topo.host(c) == topo.host(rank) and topo.chip(c) == topo.chip(rank) and c != rank
               and topo.die(c) != topo.die(rank) and topo.may_write(rank, c)
               and all(topo.may_write(c, og[e]) for e in og)][:2]

    full = topo.mask(rank, wg[1])
    for c in [wg[2], wg[3], xg[2], xg[3], og[3]]:
        full &= topo.mask(rank, c)
    ne = _count(full)
    onm = ~full
    for h in helpers:
        onm &= topo.mask(rank, h)
    non = _count(onm)
    hm = topo.mask(helpers[0], og[0])
    for h in helpers:
        for e in og:
            hm &= topo.mask(h, og[e])
    nh = _count(hm)

    if core != rank:
        if core not in helpers:
            return
        jobs = [[(0, S.la), (1, S.lb)], [(2, S.la)]][helpers.index(core)]
        g.wait_ge(S.hw, non)
        for e, sem in jobs:
            rid, pid = topo.addr(og[e], core)
            g.remote_dma(T["v%d" % e][:], T.wd[:], sem, S.sent, pid, rid, hm)
        g.wait_ge(S.sent, len(jobs) * nh)
        return

    def dst(c):
        rid, pid = topo.addr(c, core)
        return DstId(rid=rid, pnc=pid)

    def blk(d):
        return slice(d * TK, (d + 1) * TK)

    frn = slice(TK, 3 * TK)
    n2 = 2 * TK
    lo, hi = slice(0, TK), slice(TK, n2)

    g.sync.dma_start(T.xall[:, blk(0)], T.x[:]).then_inc(S.xin, 16)
    g.scalar.dma_start(T.w0[:], T.w[:]).then_inc(S.wl, 16)
    g.sync.dma_start(T.wd[:], T.w[:]).then_inc(S.wdl, 16)

    g.wait_ge(S.xin, 16)
    g.remote_dma_fused([RemoteDMATransfer(dst_ids=[dst(xg[3]), dst(xg[2])], dma_engine_mask=full, remote_sem=S.xa,
                                          srcs=[T.xall[:, blk(0)]], dsts=[T.xall[:, blk(2)], T.xall[:, blk(1)]], alu_op=0)],
                       local_sem=S.sent)
    g.wait_ge(S.wdl, 16)
    g.remote_dma_fused([RemoteDMATransfer(dst_ids=[dst(h) for h in helpers], dma_engine_mask=onm, remote_sem=S.hw,
                                          srcs=[T.wd[:]], dsts=[T.wd[:] for h in helpers], alu_op=0)], local_sem=S.sent)
    g.wait_ge(S.wl, 16)
    for c, buf, sem in ((wg[1], T.w1, S.wa), (wg[2], T.w2, S.wc), (wg[3], T.w3, S.wb), (og[3], T.v3, S.lb)):
        rid, pid = topo.addr(c, core)
        g.remote_dma(buf[:], T.w0[:], sem, S.sent, pid, rid, full)

    te = g.tensor
    xo = T.xall[:, blk(0)]
    xf = T.xall[:, frn]
    te.wait_ge(S.xin, 16)
    te.wait_ge(S.xa, 2 * ne)
    te.wait_ge(S.wl, 16)
    te.matmul(T.f0[:, 0:n2], T.w0[:], xf, start=True, stop=True).then_inc(S.mf0, 1)
    te.matmul(T.px[:, blk(0)], T.w0[:], xo, start=True, stop=True).then_inc(S.mx, 1)
    te.wait_ge(S.wa, ne)
    te.matmul(T.f1[:, 0:n2], T.w1[:], xf, start=True, stop=True).then_inc(S.mf1, 1)
    te.wait_ge(S.wc, ne)
    te.matmul(T.f2[:, 0:n2], T.w2[:], xf, start=True, stop=True).then_inc(S.mf2, 1)
    te.wait_ge(S.wb, ne)
    te.matmul(T.f3a[:, lo], T.w3[:], T.xall[:, blk(2)], start=True, stop=True).then_inc(S.mf3a, 1)
    te.matmul(T.f3b[:, lo], T.w3[:], T.xall[:, blk(1)], start=True, stop=True).then_inc(S.mf3b, 1)
    te.matmul(T.px[:, blk(1)], T.w1[:], xo, start=True, stop=True).then_inc(S.mx, 1)
    te.matmul(T.px[:, blk(2)], T.w2[:], xo, start=True, stop=True).then_inc(S.mx, 1)
    te.matmul(T.px[:, blk(3)], T.w3[:], xo, start=True, stop=True).then_inc(S.mx, 1)
    te.wait_ge(S.la, 2 * nh)
    te.matmul(T.pa[:, lo], T.v0[:], xo, start=True, stop=True).then_inc(S.ma, 1)
    te.matmul(T.pa[:, hi], T.v2[:], xo, start=True, stop=True).then_inc(S.ma, 1)
    te.wait_ge(S.lb, nh + ne)
    te.matmul(T.pb[:, lo], T.v1[:], xo, start=True, stop=True).then_inc(S.mb, 1)
    te.matmul(T.pb[:, hi], T.v3[:], xo, start=True, stop=True).then_inc(S.mb, 1)

    ve = g.vector
    mx = AluOpType.max
    ve.wait_ge(S.mf0, 1)
    ve.tensor_copy(T.a0[:], T.f0[:, 0:n2]).then_inc(S.vc, 1)
    ve.wait_ge(S.mf1, 1)
    ve.wait_ge(S.vc, 1)
    ve.tensor_tensor(T.a1[:], T.a0[:], T.f1[:, 0:n2], mx).then_inc(S.vc, 1)
    ve.wait_ge(S.mf2, 1)
    ve.wait_ge(S.vc, 2)
    ve.tensor_tensor(T.a2[:], T.a1[:], T.f2[:, 0:n2], mx).then_inc(S.vc, 1)
    ve.wait_ge(S.mf3a, 1)
    ve.wait_ge(S.vc, 3)
    ve.tensor_tensor(T.ys3[:], T.a2[:, hi], T.f3a[:, lo], mx).then_inc(S.yv3, 1)
    ve.wait_ge(S.mf3b, 1)
    ve.tensor_tensor(T.ys2[:], T.a2[:, lo], T.f3b[:, lo], mx).then_inc(S.yv2, 1)
    ve.wait_ge(S.mx, 4)
    ve.tensor_copy(T.o1[:], T.px[:, 0:n2]).then_inc(S.vo, 1)
    ve.wait_ge(S.vo, 1)
    ve.tensor_tensor(T.o2[:], T.o1[:], T.px[:, n2:2 * n2], mx).then_inc(S.vo, 1)
    ve.wait_ge(S.ma, 2)
    ve.wait_ge(S.vo, 2)
    ve.tensor_tensor(T.o3[:], T.o2[:], T.pa[:, 0:n2], mx).then_inc(S.vo, 1)
    ve.wait_ge(S.mb, 2)
    ve.wait_ge(S.vo, 3)
    ve.tensor_tensor(T.o4[:], T.o3[:], T.pb[:, 0:n2], mx).then_inc(S.vo, 1)
    ve.wait_ge(S.vo, 4)
    ve.tensor_tensor(T.own[:], T.o4[:, lo], T.o4[:, hi], mx).then_inc(S.vo, 1)

    g.wait_ge(S.yv3, 1)
    rid, pid = topo.addr(xg[3], core)
    g.remote_dma(T.yr3[:], T.ys3[:], S.ya3, S.sent, pid, rid, full)
    g.wait_ge(S.yv2, 1)
    rid, pid = topo.addr(xg[2], core)
    g.remote_dma(T.yr2[:], T.ys2[:], S.ya2, S.sent, pid, rid, full)

    ve.wait_ge(S.vo, 5)
    ve.wait_ge(S.ya3, ne)
    ve.tensor_tensor(T.t1[:], T.own[:], T.yr3[:], mx).then_inc(S.vf, 1)
    ve.wait_ge(S.ya2, ne)
    ve.wait_ge(S.vf, 1)
    ve.tensor_tensor(T.yout[:], T.t1[:], T.yr2[:], mx).then_inc(S.fin, 1)

    g.sync.wait_ge(S.fin, 1)
    g.sync.dma_start(T.y[:], T.yout[:]).then_inc(S.st, 16)
    g.sync.wait_ge(S.st, 16)
    g.wait_ge(S.sent, 7 * ne + non)
